import numpy as np
import ml_dtypes


def mxq(x, axis, fmt="e4m3"):
    dtype, down = {"e4m3": (ml_dtypes.float8_e4m3fn, 7), "e5m2": (ml_dtypes.float8_e5m2, 14)}[fmt]
    v = np.moveaxis(np.asarray(x, np.float32).astype(ml_dtypes.bfloat16).astype(np.float64), axis, -1)
    blocks = v.reshape(v.shape[:-1] + (-1, 32))
    amax = np.abs(blocks).max(-1, keepdims=True)
    byte = np.maximum(np.where(amax > 0, np.frexp(amax)[1] - 1 + 127, 0) - down, 1)
    scale = np.exp2(byte - 127.0)
    codes = (blocks / scale).astype(np.float32).astype(dtype).astype(np.float64)
    return np.moveaxis((codes * scale).reshape(v.shape), -1, axis)


WIDE = False


def mx_kscale(k):
    if not WIDE:
        return np.ones(k)
    levels = np.array([10, -10, 5, -5, 0])
    if k % 512:
        return np.exp2(np.random.permutation(np.resize(levels, k // 32))).repeat(32)
    a = np.empty((k // 512, 16))
    for p in range(k // 512):
        a[p, :8] = np.random.permutation(np.resize(levels, 8))
        for g in range(8):
            far = levels[np.abs(levels - a[p, g]) >= 10]
            a[p, g + 8] = far[np.random.randint(len(far))]
    return np.exp2(a.ravel()).repeat(32)


def f64(x):
    return np.asarray(x).astype(np.float64)


def striped(idx):
    return np.tile(idx.reshape(-1, 16).T, (8, 1)).astype(np.uint16)


def unstriped(offs):
    return offs[:16].T.reshape(-1).astype(np.int64)


def striped8(idx):
    return np.concatenate([x.reshape(-1, 16).T for x in idx]).astype(np.uint16)


def runs(offs, k):
    lists = np.stack([offs[16 * r : 16 * r + 16].T.reshape(-1) for r in range(8)]).astype(np.int64)
    return lists[np.arange(k) % 512 // 64]


def pack_weight(w):
    k, n = w.shape
    w = f64(np.asarray(w, np.float32).astype(ml_dtypes.bfloat16)).reshape(k // 32, 32, n)
    amax = np.abs(w).max(1)
    byte = np.clip(np.where(amax > 0, np.frexp(amax)[1] - 1 + 127 - 7, 1), 1, 254)
    scaled = (w * np.exp2(127.0 - byte)[:, None, :]).reshape(k, n).astype(np.float32)
    words = np.ascontiguousarray(scaled.reshape(k // 512, 128, 4, n).transpose(0, 1, 3, 2)).astype(ml_dtypes.float8_e4m3fn).view(np.uint8)
    return words, np.ascontiguousarray(byte.astype(np.uint8).reshape(k // 512, 16, n))


def unpack_weight(words, scales):
    g, p, n, _ = words.shape
    vals = np.ascontiguousarray(words).view(ml_dtypes.float8_e4m3fn).astype(np.float64) * np.repeat(np.exp2(scales.astype(np.float64) - 127.0), 8, axis=1)[..., None]
    return vals.transpose(0, 1, 3, 2).reshape(g * 512, n)

def planes(y):
    n, m = y.shape
    v = y.astype(np.float32).astype(ml_dtypes.bfloat16).astype(np.float64).reshape(n // 32, 32, m)
    top = np.abs(v).max(1)
    byte = np.clip(np.where(top > 0, np.frexp(top)[1] - 1 + 127 - 7, 1), 1, 254)
    codes = (v * np.exp2(127.0 - byte)[:, None, :]).reshape(n, m).astype(np.float32).astype(ml_dtypes.float8_e4m3fn).view(np.uint8)
    words = codes.reshape(n // 512, 128, 4, m).transpose(0, 1, 3, 2)
    return np.ascontiguousarray(words), np.ascontiguousarray(byte.astype(np.uint8).reshape(n // 512, 16, m))


K, T, S, N, G, H = 512, 2048, 512, 512, 2048, 512


def setup_inputs():
    n = np.random.standard_normal
    s = mx_kscale(K)[:, None]
    u = mx_kscale(S)
    packed_xT = pack_weight(n((K, T)) * s)
    packed_dT = pack_weight(n((K, G)) / s)
    packed_w1 = pack_weight(n((H, N)) / np.sqrt(H) / u[:, None])
    return {
        "x_words": packed_xT[0],
        "x_scales": packed_xT[1],
        "d_words": packed_dT[0],
        "d_scales": packed_dT[1],
        "gn": (np.random.uniform(0.5, 1.5, (H, 1)) * u[:, None]).astype(np.float32),
        "w1_words": packed_w1[0],
        "w1_scales": packed_w1[1],
        "offs": striped(np.random.permutation(T)[:S]),
        "k1": striped8(np.random.randint(0, G, (8, H))),
        "n1": striped(np.random.permutation(S)),
        "n2": striped8(np.stack([np.random.permutation(S) for _ in range(8)])),
        "n3": striped8(np.stack([np.random.permutation(S) for _ in range(8)])),
    }


def reference(x_words, x_scales, d_words, d_scales, gn, w1_words, w1_scales, offs, k1, n1, n2, n3):
    d_k1 = unpack_weight(d_words, d_scales)[np.arange(K)[:, None], runs(k1, K)]
    xq = unpack_weight(x_words, x_scales)[:, unstriped(offs)]
    h = 0.0625 * (d_k1.T @ xq)
    pa = h[:, unstriped(n1)]
    z = f64(gn) * ((2.0 * (h * pa)) / ((h) ** 2 + (pa) ** 2 + 0.5))
    h2 = unpack_weight(w1_words, w1_scales).T @ mxq(z, 0, "e4m3")
    out_0 = (h2[np.arange(N)[:, None], runs(n2, N)]) * (h2[np.arange(N)[:, None], runs(n3, N)])
    return (out_0,) + planes(out_0)

@@ -1,0 +1,271 @@
+from contextlib import ExitStack
+
+import concourse.mybir as mybir
+
+K, T, S, N, G, H = 512, 2048, 512, 512, 2048, 512
+FLOPS = 2 * K * H * S + 2 * H * N * S
+
+F32 = mybir.dt.float32
+BF16 = mybir.dt.bfloat16
+I32 = mybir.dt.int32
+U32 = mybir.dt.uint32
+U16 = mybir.dt.uint16
+U8 = mybir.dt.uint8
+FP8X4 = mybir.dt.float8_e4m3fn_x4
+ACT = mybir.ActivationFunctionType
+ALU = mybir.AluOpType
+
+P = 128
+PACK = 4
+Z_CHUNK = 128
+O_CHUNK = 256
+HALF = 256
+
+
+def words_of(dram):
+    return dram[0].rearrange("p n r -> p (n r)").bitcast(I32)
+
+
+def entries(offsets, start, count):
+    return offsets[:, start // 16 : (start + count) // 16]
+
+
+def tile_picked_pqlayharmprod_none_po_kernel(
+    tc, x_words, x_scales, d_words, d_scales, gn, w1_words, w1_scales, offs, k1, n1, n2, n3, out_0, out_1, out_2
+):
+    nc = tc.nc
+    with ExitStack() as ctx:
+        held = ctx.enter_context(tc.tile_pool(name="held", bufs=1))
+        work = ctx.enter_context(tc.tile_pool(name="work", bufs=1))
+        psum = ctx.enter_context(tc.psum_pool(name="psum", bufs=1))
+
+        k1_sb = held.tile([P, H // 16], U16, name="k1_sb")
+        offs_sb = held.tile([P, S // 16], U16, name="offs_sb")
+        n1_sb = held.tile([P, S // 16], U16, name="n1_sb")
+        n2_sb = held.tile([P, S // 16], U16, name="n2_sb")
+        n3_sb = held.tile([P, S // 16], U16, name="n3_sb")
+
+        d_scale_tab = work.tile([P, G], U8, name="d_scale_tab")
+        x_scale_tab = work.tile([P, T], U8, name="x_scale_tab")
+        d_word_tab = work.tile([P, G], U32, name="d_word_tab", tag="table")
+        x_word_tab = work.tile([P, T], U32, name="x_word_tab")
+        w_scale_raw = work.tile([P, N], U8, name="w_scale_raw")
+
+        nc.vector.memset(d_scale_tab[:].bitcast(I32), 0)
+        nc.vector.memset(x_scale_tab[:].bitcast(I32), 0)
+        nc.vector.memset(w_scale_raw[:].bitcast(I32), 0)
+
+        nc.sync.dma_start(k1_sb[:], k1)
+        nc.scalar.dma_start(d_scale_tab[0:P:8, :].bitcast(I32), d_scales[0].bitcast(I32))
+        nc.sync.dma_start(offs_sb[:], offs)
+        nc.sync.dma_start(d_word_tab[:].bitcast(I32), words_of(d_words))
+        nc.sync.dma_start(n1_sb[:], n1)
+        nc.sync.dma_start(x_word_tab[:].bitcast(I32), words_of(x_words))
+        nc.sync.dma_start(n2_sb[:], n2)
+        nc.sync.dma_start(n3_sb[:], n3)
+        for q in range(4):
+            nc.gpsimd.dma_start(x_scale_tab[32 * q : 32 * q + 4, :].bitcast(I32), x_scales[0][4 * q : 4 * q + 4, :].bitcast(I32))
+        for q in range(4):
+            nc.gpsimd.dma_start(w_scale_raw[32 * q : 32 * q + 4, :].bitcast(I32), w1_scales[0][4 * q : 4 * q + 4, :].bitcast(I32))
+
+        d_scale_got = work.tile([P, H], U8, name="d_scale_got", tag="small")
+        nc.vector.tensor_copy(d_scale_got[:], d_scale_tab[:].indirect(k1_sb[:]))
+        d_scale_dealt = work.tile([P, H], U8, name="d_scale_dealt")
+        nc.vector.tensor_copy(
+            d_scale_dealt[:].rearrange("p (t m) -> p t m", t=PACK), d_scale_got[:].rearrange("p (m t) -> p t m", t=PACK)
+        )
+        d_scale = work.tile([P, H], U8, name="d_scale", align_bytes=64)
+        nc.vector.tensor_copy(d_scale[:].bitcast(I32), d_scale_dealt[:].bitcast(I32))
+        for j in range(1, 4):
+            nc.scalar.dma_start(d_scale[j:P:32, :].bitcast(I32), d_scale_dealt[8 * j : P : 32, :].bitcast(I32))
+
+        d_word_got = work.tile([P, H], U32, name="d_word_got")
+        nc.vector.tensor_copy(d_word_got[:], d_word_tab[:].indirect(k1_sb[:]))
+        d_word = work.tile([P, H], U32, name="d_word", align_bytes=64)
+        nc.vector.tensor_copy(
+            d_word[:].rearrange("p (t m) -> p t m", t=PACK), d_word_got[:].rearrange("p (m t) -> p t m", t=PACK)
+        )
+        x_scale = work.tile([P, S], U8, name="x_scale", align_bytes=64)
+        nc.vector.tensor_copy(x_scale[:], x_scale_tab[:].indirect(offs_sb[:]))
+
+        x_word = [work.tile([P, HALF], U32, name=f"x_word{u}", align_bytes=64) for u in range(2)]
+        for u in range(2):
+            nc.vector.tensor_copy(x_word[u][:], x_word_tab[:].indirect(entries(offs_sb, u * HALF, HALF)))
+
+        w_word_raw = work.tile([P, N], U32, name="w_word_raw", tag="table")
+        nc.sync.dma_start(w_word_raw[:].bitcast(I32), words_of(w1_words))
+        gain = work.tile([P, PACK], F32, name="gain", tag="small")
+        nc.sync.dma_start(gain[:], gn.rearrange("(p t) o -> p (t o)", t=PACK))
+
+        w_word = work.tile([P, N], U32, name="w_word", align_bytes=64)
+        nc.gpsimd.tensor_copy(
+            w_word[:].rearrange("p (t m) -> p t m", t=PACK), w_word_raw[:].rearrange("p (m t) -> p t m", t=PACK)
+        )
+        w_scale = work.tile([P, N], U8, name="w_scale", align_bytes=64)
+        nc.gpsimd.tensor_copy(
+            w_scale[:].rearrange("p (t m) -> p t m", t=PACK), w_scale_raw[:].rearrange("p (m t) -> p t m", t=PACK)
+        )
+
+        h_ps = {}
+        for pair in range(2):
+            for u in range(2):
+                for t in (2 * pair, 2 * pair + 1):
+                    cols = slice(P * t, P * (t + 1))
+                    h_ps[t, u] = psum.tile([P, HALF], F32, name=f"h_ps{t}{u}", tag=f"bank{t}{u}")
+                    nc.tensor.matmul_mx(
+                        out=h_ps[t, u][:], lhsT=d_word[:, cols].bitcast(FP8X4), lhsT_scale=d_scale[:, cols],
+                        rhs=x_word[u][:].bitcast(FP8X4), rhs_scale=x_scale[:, u * HALF : (u + 1) * HALF], start=True, stop=True,
+                    )
+
+        h_sb = work.tile([P, PACK, S], F32, name="h_sb")
+        h2_sb = [work.tile([P, S], F32, name=f"h2_sb{t}") for t in range(PACK)]
+        pa = [work.tile([P, PACK, HALF], F32, name=f"pa{u}") for u in range(S // HALF)]
+        chunks = S // Z_CHUNK
+        h_sq = [work.tile([P, PACK, Z_CHUNK], F32, name=f"h_sq{c}") for c in range(chunks)]
+        pa_sq = [work.tile([P, PACK, Z_CHUNK], F32, name=f"pa_sq{c}") for c in range(chunks)]
+        den = [work.tile([P, PACK, Z_CHUNK], F32, name=f"den{c}") for c in range(chunks)]
+        root = [work.tile([P, PACK, Z_CHUNK], F32, name=f"root{c}") for c in range(chunks)]
+        inv = [work.tile([P, PACK, Z_CHUNK], F32, name=f"inv{c}") for c in range(chunks)]
+        prod = [work.tile([P, PACK, Z_CHUNK], F32, name=f"prod{c}") for c in range(chunks)]
+        h2_ps = {}
+
+        def cols_of(c):
+            return slice(c * Z_CHUNK, (c + 1) * Z_CHUNK)
+
+        def pa_of(c):
+            start = c * Z_CHUNK % HALF
+            return pa[c * Z_CHUNK // HALF][:, :, start : start + Z_CHUNK]
+
+        def fetch(t, u, on_vector):
+            window = h_sb[:, t, :].indirect(entries(n1_sb, u * HALF, HALF))
+            if on_vector:
+                nc.vector.tensor_copy(pa[u][:, t, :], window)
+            else:
+                nc.scalar.activation(pa[u][:, t, :], window, ACT.Copy)
+
+        def square_h(c):
+            nc.scalar.activation(h_sq[c][:], h_sb[:, :, cols_of(c)], ACT.Square)
+
+        def square_pa(c):
+            nc.scalar.activation(pa_sq[c][:], pa_of(c), ACT.Square)
+
+        def add_squares(c):
+            nc.vector.tensor_tensor(den[c][:], h_sq[c][:], pa_sq[c][:], ALU.add)
+
+        def inverse_root(c):
+            nc.scalar.activation(root[c][:], den[c][:], ACT.Abs_reciprocal_sqrt, bias=64.0, scale=0.5)
+
+        def inverse(c):
+            nc.scalar.activation(inv[c][:], root[c][:], ACT.Square)
+
+        def product(c):
+            for t in range(PACK):
+                nc.vector.scalar_tensor_tensor(
+                    prod[c][:, t, :], h_sb[:, t, cols_of(c)], gain[:, t : t + 1], pa_of(c)[:, t, :], ALU.mult, ALU.mult
+                )
+
+        z = [work.tile([P, Z_CHUNK * PACK], BF16, name=f"z{c}", align_bytes=64) for c in range(chunks)]
+
+        def round_z(c):
+            nc.vector.tensor_tensor(
+                z[c][:].rearrange("p (g i t) -> p g t i", i=4, t=PACK),
+                prod[c][:].rearrange("p t (g i) -> p g t i", i=4),
+                inv[c][:].rearrange("p t (g i) -> p g t i", i=4),
+                ALU.mult,
+            )
+
+        def second_layer(c):
+            z_word = work.tile([P, Z_CHUNK], U32, name=f"z_word{c}", align_bytes=64)
+            z_scale = work.tile([P, Z_CHUNK], U8, name=f"z_scale{c}", align_bytes=64)
+            nc.vector.quantize_mx(out=z_word[:].bitcast(FP8X4), scales=z_scale[:], in_=z[c][:])
+            u, start = divmod(c * Z_CHUNK, HALF)
+            for t in range(PACK):
+                wc = slice(P * t, P * (t + 1))
+                if start == 0:
+                    h2_ps[t, u] = psum.tile([P, HALF], F32, name=f"h2_ps{t}{u}", tag=f"bank{t}{u}")
+                nc.tensor.matmul_mx(
+                    out=h2_ps[t, u][:, start : start + Z_CHUNK], lhsT=w_word[:, wc].bitcast(FP8X4), lhsT_scale=w_scale[:, wc],
+                    rhs=z_word[:].bitcast(FP8X4), rhs_scale=z_scale[:], start=True, stop=True,
+                )
+
+        for pair in range(2):
+            for t in (2 * pair, 2 * pair + 1):
+                nc.scalar.copy(h_sb[:, t, 0:HALF], h_ps[t, 0][:])
+            for t in (2 * pair, 2 * pair + 1):
+                nc.vector.tensor_copy(h_sb[:, t, HALF:S], h_ps[t, 1][:])
+            for t in (2 * pair, 2 * pair + 1):
+                fetch(t, 0, True)
+        square_h(0)
+        square_h(1)
+        for t in range(PACK):
+            fetch(t, 1, t == PACK - 1)
+        square_pa(0)
+        product(0)
+        add_squares(0)
+        square_pa(1)
+        product(1)
+        add_squares(1)
+        square_h(2)
+        square_pa(2)
+        inverse_root(0)
+        add_squares(2)
+        inverse_root(1)
+        square_h(3)
+        square_pa(3)
+        inverse(0)
+        add_squares(3)
+        inverse(1)
+        product(2)
+        round_z(0)
+        inverse_root(2)
+        second_layer(0)
+        round_z(1)
+        inverse_root(3)
+        product(3)
+        second_layer(1)
+        inverse(2)
+        inverse(3)
+        round_z(2)
+        round_z(3)
+        second_layer(2)
+        second_layer(3)
+        for t in range(PACK):
+            nc.scalar.copy(h2_sb[t][:, 0:HALF], h2_ps[t, 0][:])
+        for t in range(PACK):
+            if t % 2 == 0:
+                nc.scalar.copy(h2_sb[t][:, HALF:S], h2_ps[t, 1][:])
+            else:
+                nc.vector.tensor_copy(h2_sb[t][:, HALF:S], h2_ps[t, 1][:])
+
+        out_rows = out_0.rearrange("(p t) j -> p t j", t=PACK)
+        y_word = work.tile([P, S], U32, name="y_word", align_bytes=64)
+        y_scale = work.tile([P, S], U8, name="y_scale", align_bytes=64)
+        left = {}
+        for u in range(2):
+            for t in range(PACK):
+                left[t, u] = work.tile([P, HALF], F32, name=f"left{t}{u}")
+                window = h2_sb[t][:].indirect(entries(n2_sb, u * HALF, HALF))
+                if (t, u) == (1, 0):
+                    nc.vector.tensor_copy(left[t, u][:], window)
+                else:
+                    nc.scalar.activation(left[t, u][:], window, ACT.Copy)
+        y = [work.tile([P, PACK, HALF], F32, name=f"y{u}") for u in range(2)]
+        for u in range(2):
+            for t in range(PACK):
+                nc.vector.tensor_tensor(y[u][:, t, :], h2_sb[t][:].indirect(entries(n3_sb, u * HALF, HALF)), left[t, u][:], ALU.mult)
+                if t % 2 == 1:
+                    nc.sync.dma_start(out_rows[:, t - 1 : t + 1, u * HALF : (u + 1) * HALF], y[u][:, t - 1 : t + 1, :])
+        for u in range(2):
+            cols = slice(u * HALF, (u + 1) * HALF)
+            y_bf = work.tile([P, HALF * PACK], BF16, name=f"y_bf{u}", align_bytes=64)
+            woven = y_bf[:].rearrange("p (g i t) -> p g t i", i=4, t=PACK)
+            planes = y[u][:].rearrange("p t (g i) -> p g t i", i=4)
+            if u == 0:
+                nc.scalar.copy(woven, planes)
+            else:
+                nc.vector.tensor_copy(woven, planes)
+            nc.vector.quantize_mx(out=y_word[:, cols].bitcast(FP8X4), scales=y_scale[:, cols], in_=y_bf[:])
+            nc.sync.dma_start(words_of(out_1)[:, cols], y_word[:, cols].bitcast(I32))
+        for q in range(4):
+            queue = nc.sync if q % 2 == 0 else nc.scalar
+            queue.dma_start(out_2[0][4 * q : 4 * q + 4, :].bitcast(I32), y_scale[32 * q : 32 * q + 4, :].bitcast(I32))

@@ -46,57 +46,61 @@ def tile_picked_pqlayharmprod_none_po_kernel(
         n3_sb = held.tile([P, S // 16], U16, name="n3_sb")
 
         d_scale_tab = work.tile([P, G], U8, name="d_scale_tab")
-        x_scale_tab = work.tile([P, T], U8, name="x_scale_tab")
-        d_word_tab = work.tile([P, G], U32, name="d_word_tab", tag="table")
+        x_scale_tab = work.tile([P, T], U8, name="x_scale_tab", tag="scales")
+        d_word_tab = work.tile([P, G], U32, name="d_word_tab", tag="words")
         x_word_tab = work.tile([P, T], U32, name="x_word_tab")
         w_scale_raw = work.tile([P, N], U8, name="w_scale_raw")
 
-        nc.vector.memset(d_scale_tab[:].bitcast(I32), 0)
-        nc.vector.memset(x_scale_tab[:].bitcast(I32), 0)
-        nc.vector.memset(w_scale_raw[:].bitcast(I32), 0)
+        d_scale = work.tile([P, H], U8, name="d_scale", align_bytes=64)
+        for tab in (d_scale_tab, x_scale_tab):
+            nc.vector.memset(tab[:, 0 : T // 2].bitcast(I32), 0)
+            nc.gpsimd.memset(tab[:, T // 2 : T].bitcast(I32), 0)
+        nc.vector.memset(d_scale[:].bitcast(I32), 0)
+        nc.gpsimd.memset(w_scale_raw[:].bitcast(I32), 0)
 
         nc.sync.dma_start(k1_sb[:], k1)
-        nc.scalar.dma_start(d_scale_tab[0:P:8, :].bitcast(I32), d_scales[0].bitcast(I32))
+        nc.sync.dma_start(d_scale_tab[0:P:8, :].bitcast(I32), d_scales[0].bitcast(I32))
         nc.sync.dma_start(offs_sb[:], offs)
+        for q in range(4):
+            nc.sync.dma_start(x_scale_tab[32 * q : 32 * q + 4, :].bitcast(I32), x_scales[0][4 * q : 4 * q + 4, :].bitcast(I32))
         nc.sync.dma_start(d_word_tab[:].bitcast(I32), words_of(d_words))
-        nc.sync.dma_start(n1_sb[:], n1)
         nc.sync.dma_start(x_word_tab[:].bitcast(I32), words_of(x_words))
+        warm_in = work.tile([P, 1], F32, name="warm_in")
+        warm_out = work.tile([P, 1], F32, name="warm_out")
+        nc.gpsimd.memset(warm_in[:], 1.0)
+        nc.scalar.activation(warm_out[:], warm_in[:], ACT.Abs_reciprocal_sqrt)
+
+        nc.sync.dma_start(n1_sb[:], n1)
         nc.sync.dma_start(n2_sb[:], n2)
         nc.sync.dma_start(n3_sb[:], n3)
+        gain = work.tile([P, PACK], F32, name="gain")
+        nc.sync.dma_start(gain[:], gn.rearrange("(p t) o -> p (t o)", t=PACK))
         for q in range(4):
-            nc.gpsimd.dma_start(x_scale_tab[32 * q : 32 * q + 4, :].bitcast(I32), x_scales[0][4 * q : 4 * q + 4, :].bitcast(I32))
-        for q in range(4):
-            nc.gpsimd.dma_start(w_scale_raw[32 * q : 32 * q + 4, :].bitcast(I32), w1_scales[0][4 * q : 4 * q + 4, :].bitcast(I32))
+            nc.sync.dma_start(w_scale_raw[32 * q : 32 * q + 4, :].bitcast(I32), w1_scales[0][4 * q : 4 * q + 4, :].bitcast(I32))
 
-        d_scale_got = work.tile([P, H], U8, name="d_scale_got", tag="small")
+        d_scale_got = work.tile([P, H], U8, name="d_scale_got")
         nc.vector.tensor_copy(d_scale_got[:], d_scale_tab[:].indirect(k1_sb[:]))
-        d_scale_dealt = work.tile([P, H], U8, name="d_scale_dealt")
+        x_scale = work.tile([P, S], U8, name="x_scale", align_bytes=64)
+        nc.vector.tensor_copy(x_scale[:], x_scale_tab[:].indirect(offs_sb[:]))
+        d_scale_dealt = work.tile([P, H], U8, name="d_scale_dealt", tag="scales")
         nc.vector.tensor_copy(
-            d_scale_dealt[:].rearrange("p (t m) -> p t m", t=PACK), d_scale_got[:].rearrange("p (m t) -> p t m", t=PACK)
+            d_scale_dealt[:].rearrange("p (t m) -> p m t", t=PACK), d_scale_got[:].rearrange("p (m t) -> p m t", t=PACK)
         )
-        d_scale = work.tile([P, H], U8, name="d_scale", align_bytes=64)
-        nc.vector.tensor_copy(d_scale[:].bitcast(I32), d_scale_dealt[:].bitcast(I32))
-        for j in range(1, 4):
+        for j in range(4):
             nc.scalar.dma_start(d_scale[j:P:32, :].bitcast(I32), d_scale_dealt[8 * j : P : 32, :].bitcast(I32))
 
         d_word_got = work.tile([P, H], U32, name="d_word_got")
         nc.vector.tensor_copy(d_word_got[:], d_word_tab[:].indirect(k1_sb[:]))
         d_word = work.tile([P, H], U32, name="d_word", align_bytes=64)
         nc.vector.tensor_copy(
-            d_word[:].rearrange("p (t m) -> p t m", t=PACK), d_word_got[:].rearrange("p (m t) -> p t m", t=PACK)
+            d_word[:].rearrange("p (t m) -> p m t", t=PACK), d_word_got[:].rearrange("p (m t) -> p m t", t=PACK)
         )
-        x_scale = work.tile([P, S], U8, name="x_scale", align_bytes=64)
-        nc.vector.tensor_copy(x_scale[:], x_scale_tab[:].indirect(offs_sb[:]))
-
         x_word = [work.tile([P, HALF], U32, name=f"x_word{u}", align_bytes=64) for u in range(2)]
         for u in range(2):
             nc.vector.tensor_copy(x_word[u][:], x_word_tab[:].indirect(entries(offs_sb, u * HALF, HALF)))
 
-        w_word_raw = work.tile([P, N], U32, name="w_word_raw", tag="table")
-        nc.sync.dma_start(w_word_raw[:].bitcast(I32), words_of(w1_words))
-        gain = work.tile([P, PACK], F32, name="gain", tag="small")
-        nc.sync.dma_start(gain[:], gn.rearrange("(p t) o -> p (t o)", t=PACK))
-
+        w_word_raw = work.tile([P, N], U32, name="w_word_raw", tag="words")
+        nc.scalar.dma_start(w_word_raw[:].bitcast(I32), words_of(w1_words))
         w_word = work.tile([P, N], U32, name="w_word", align_bytes=64)
         nc.gpsimd.tensor_copy(
             w_word[:].rearrange("p (t m) -> p t m", t=PACK), w_word_raw[:].rearrange("p (m t) -> p t m", t=PACK)
@@ -198,37 +202,27 @@ def tile_picked_pqlayharmprod_none_po_kernel(
         square_h(0)
         square_h(1)
         for t in range(PACK):
-            fetch(t, 1, t == PACK - 1)
+            fetch(t, 1, t >= 2)
         square_pa(0)
-        product(0)
-        add_squares(0)
         square_pa(1)
-        product(1)
+        add_squares(0)
         add_squares(1)
         square_h(2)
+        square_h(3)
         square_pa(2)
+        square_pa(3)
         inverse_root(0)
         add_squares(2)
-        inverse_root(1)
-        square_h(3)
-        square_pa(3)
-        inverse(0)
         add_squares(3)
-        inverse(1)
-        product(2)
-        round_z(0)
-        inverse_root(2)
-        second_layer(0)
-        round_z(1)
-        inverse_root(3)
-        product(3)
-        second_layer(1)
-        inverse(2)
-        inverse(3)
-        round_z(2)
-        round_z(3)
-        second_layer(2)
-        second_layer(3)
+        for c in range(chunks):
+            if c + 1 < chunks:
+                inverse_root(c + 1)
+            inverse(c)
+            product(c)
+            if c > 0:
+                second_layer(c - 1)
+            round_z(c)
+        second_layer(chunks - 1)
         for t in range(PACK):
             nc.scalar.copy(h2_sb[t][:, 0:HALF], h2_ps[t, 0][:])
         for t in range(PACK):
@@ -263,7 +257,8 @@ def tile_picked_pqlayharmprod_none_po_kernel(
             if u == 0:
                 nc.scalar.copy(woven, planes)
             else:
-                nc.vector.tensor_copy(woven, planes)
+                nc.vector.tensor_copy(woven[:, 0:48], planes[:, 0:48])
+                nc.scalar.copy(woven[:, 48:64], planes[:, 48:64])
             nc.vector.quantize_mx(out=y_word[:, cols].bitcast(FP8X4), scales=y_scale[:, cols], in_=y_bf[:])
             nc.sync.dma_start(words_of(out_1)[:, cols], y_word[:, cols].bitcast(I32))
         for q in range(4):

@@ -37,6 +37,7 @@ def tile_picked_pqlayharmprod_none_po_kernel(
     with ExitStack() as ctx:
         held = ctx.enter_context(tc.tile_pool(name="held", bufs=1))
         work = ctx.enter_context(tc.tile_pool(name="work", bufs=1))
+        reused = ctx.enter_context(tc.tile_pool(name="reused", bufs=1))
         psum = ctx.enter_context(tc.psum_pool(name="psum", bufs=1))
 
         k1_sb = held.tile([P, H // 16], U16, name="k1_sb")
@@ -46,28 +47,25 @@ def tile_picked_pqlayharmprod_none_po_kernel(
         n3_sb = held.tile([P, S // 16], U16, name="n3_sb")
 
         d_scale_tab = work.tile([P, G], U8, name="d_scale_tab")
-        x_scale_tab = work.tile([P, T], U8, name="x_scale_tab", tag="scales")
-        d_word_tab = work.tile([P, G], U32, name="d_word_tab", tag="words")
+        x_scale_tab = work.tile([P, T], U8, name="x_scale_tab")
+        d_word_tab = reused.tile([P, G], U32, name="d_word_tab", offset=0)
         x_word_tab = work.tile([P, T], U32, name="x_word_tab")
         w_scale_raw = work.tile([P, N], U8, name="w_scale_raw")
 
         d_scale = work.tile([P, H], U8, name="d_scale", align_bytes=64)
-        for tab in (d_scale_tab, x_scale_tab):
-            nc.vector.memset(tab[:, 0 : T // 2].bitcast(I32), 0)
-            nc.gpsimd.memset(tab[:, T // 2 : T].bitcast(I32), 0)
-        nc.vector.memset(d_scale[:].bitcast(I32), 0)
-        nc.gpsimd.memset(w_scale_raw[:].bitcast(I32), 0)
+        for plane in (d_scale_tab, x_scale_tab, d_scale, w_scale_raw):
+            nc.vector.memset(plane[:].bitcast(I32), 0)
 
         nc.sync.dma_start(k1_sb[:], k1)
         nc.sync.dma_start(d_scale_tab[0:P:8, :].bitcast(I32), d_scales[0].bitcast(I32))
         nc.sync.dma_start(offs_sb[:], offs)
         for q in range(4):
-            nc.sync.dma_start(x_scale_tab[32 * q : 32 * q + 4, :].bitcast(I32), x_scales[0][4 * q : 4 * q + 4, :].bitcast(I32))
+            nc.scalar.dma_start(x_scale_tab[32 * q : 32 * q + 4, :].bitcast(I32), x_scales[0][4 * q : 4 * q + 4, :].bitcast(I32))
         nc.sync.dma_start(d_word_tab[:].bitcast(I32), words_of(d_words))
         nc.sync.dma_start(x_word_tab[:].bitcast(I32), words_of(x_words))
         warm_in = work.tile([P, 1], F32, name="warm_in")
         warm_out = work.tile([P, 1], F32, name="warm_out")
-        nc.gpsimd.memset(warm_in[:], 1.0)
+        nc.vector.memset(warm_in[:], 1.0)
         nc.scalar.activation(warm_out[:], warm_in[:], ACT.Abs_reciprocal_sqrt)
 
         nc.sync.dma_start(n1_sb[:], n1)
@@ -80,9 +78,7 @@ def tile_picked_pqlayharmprod_none_po_kernel(
 
         d_scale_got = work.tile([P, H], U8, name="d_scale_got")
         nc.vector.tensor_copy(d_scale_got[:], d_scale_tab[:].indirect(k1_sb[:]))
-        x_scale = work.tile([P, S], U8, name="x_scale", align_bytes=64)
-        nc.vector.tensor_copy(x_scale[:], x_scale_tab[:].indirect(offs_sb[:]))
-        d_scale_dealt = work.tile([P, H], U8, name="d_scale_dealt", tag="scales")
+        d_scale_dealt = work.tile([P, H], U8, name="d_scale_dealt")
         nc.vector.tensor_copy(
             d_scale_dealt[:].rearrange("p (t m) -> p m t", t=PACK), d_scale_got[:].rearrange("p (m t) -> p m t", t=PACK)
         )
@@ -91,6 +87,8 @@ def tile_picked_pqlayharmprod_none_po_kernel(
 
         d_word_got = work.tile([P, H], U32, name="d_word_got")
         nc.vector.tensor_copy(d_word_got[:], d_word_tab[:].indirect(k1_sb[:]))
+        x_scale = reused.tile([P, S], U8, name="x_scale", align_bytes=64, offset=4 * N)
+        nc.vector.tensor_copy(x_scale[:], x_scale_tab[:].indirect(offs_sb[:]))
         d_word = work.tile([P, H], U32, name="d_word", align_bytes=64)
         nc.vector.tensor_copy(
             d_word[:].rearrange("p (t m) -> p m t", t=PACK), d_word_got[:].rearrange("p (m t) -> p m t", t=PACK)
@@ -99,7 +97,7 @@ def tile_picked_pqlayharmprod_none_po_kernel(
         for u in range(2):
             nc.vector.tensor_copy(x_word[u][:], x_word_tab[:].indirect(entries(offs_sb, u * HALF, HALF)))
 
-        w_word_raw = work.tile([P, N], U32, name="w_word_raw", tag="words")
+        w_word_raw = reused.tile([P, N], U32, name="w_word_raw", offset=0)
         nc.scalar.dma_start(w_word_raw[:].bitcast(I32), words_of(w1_words))
         w_word = work.tile([P, N], U32, name="w_word", align_bytes=64)
         nc.gpsimd.tensor_copy(

from contextlib import ExitStack

import concourse.mybir as mybir

K, T, S, N, G, H = 512, 2048, 512, 512, 2048, 512
FLOPS = 2 * K * H * S + 2 * H * N * S

F32 = mybir.dt.float32
BF16 = mybir.dt.bfloat16
I32 = mybir.dt.int32
U32 = mybir.dt.uint32
U16 = mybir.dt.uint16
U8 = mybir.dt.uint8
FP8X4 = mybir.dt.float8_e4m3fn_x4
ACT = mybir.ActivationFunctionType
ALU = mybir.AluOpType

P = 128
PACK = 4
Z_CHUNK = 128
O_CHUNK = 256
HALF = 256


def words_of(dram):
    return dram[0].rearrange("p n r -> p (n r)").bitcast(I32)


def entries(offsets, start, count):
    return offsets[:, start // 16 : (start + count) // 16]


def tile_picked_pqlayharmprod_none_po_kernel(
    tc, x_words, x_scales, d_words, d_scales, gn, w1_words, w1_scales, offs, k1, n1, n2, n3, out_0, out_1, out_2
):
    nc = tc.nc
    with ExitStack() as ctx:
        held = ctx.enter_context(tc.tile_pool(name="held", bufs=1))
        work = ctx.enter_context(tc.tile_pool(name="work", bufs=1))
        reused = ctx.enter_context(tc.tile_pool(name="reused", bufs=1))
        psum = ctx.enter_context(tc.psum_pool(name="psum", bufs=1))

        k1_sb = held.tile([P, H // 16], U16, name="k1_sb")
        offs_sb = held.tile([P, S // 16], U16, name="offs_sb")
        n1_sb = held.tile([P, S // 16], U16, name="n1_sb")
        n2_sb = held.tile([P, S // 16], U16, name="n2_sb")
        n3_sb = held.tile([P, S // 16], U16, name="n3_sb")

        d_scale_tab = work.tile([P, G], U8, name="d_scale_tab")
        x_scale_tab = work.tile([P, T], U8, name="x_scale_tab")
        d_word_tab = reused.tile([P, G], U32, name="d_word_tab", offset=0)
        x_word_tab = work.tile([P, T], U32, name="x_word_tab")
        w_scale_raw = work.tile([P, N], U8, name="w_scale_raw")

        d_scale = work.tile([P, H], U8, name="d_scale", align_bytes=64)
        for plane in (d_scale_tab, x_scale_tab, d_scale, w_scale_raw):
            nc.vector.memset(plane[:].bitcast(I32), 0)

        nc.sync.dma_start(k1_sb[:], k1)
        nc.sync.dma_start(d_scale_tab[0:P:8, :].bitcast(I32), d_scales[0].bitcast(I32))
        nc.sync.dma_start(offs_sb[:], offs)
        for q in range(4):
            nc.scalar.dma_start(x_scale_tab[32 * q : 32 * q + 4, :].bitcast(I32), x_scales[0][4 * q : 4 * q + 4, :].bitcast(I32))
        nc.sync.dma_start(d_word_tab[:].bitcast(I32), words_of(d_words))
        nc.sync.dma_start(x_word_tab[:].bitcast(I32), words_of(x_words))
        warm_in = work.tile([P, 1], F32, name="warm_in")
        warm_out = work.tile([P, 1], F32, name="warm_out")
        nc.vector.memset(warm_in[:], 1.0)
        nc.scalar.activation(warm_out[:], warm_in[:], ACT.Abs_reciprocal_sqrt)

        nc.sync.dma_start(n1_sb[:], n1)
        nc.sync.dma_start(n2_sb[:], n2)
        nc.sync.dma_start(n3_sb[:], n3)
        gain = work.tile([P, PACK], F32, name="gain")
        nc.sync.dma_start(gain[:], gn.rearrange("(p t) o -> p (t o)", t=PACK))
        for q in range(4):
            nc.sync.dma_start(w_scale_raw[32 * q : 32 * q + 4, :].bitcast(I32), w1_scales[0][4 * q : 4 * q + 4, :].bitcast(I32))

        d_scale_got = work.tile([P, H], U8, name="d_scale_got")
        nc.vector.tensor_copy(d_scale_got[:], d_scale_tab[:].indirect(k1_sb[:]))
        d_scale_dealt = work.tile([P, H], U8, name="d_scale_dealt")
        nc.vector.tensor_copy(
            d_scale_dealt[:].rearrange("p (t m) -> p m t", t=PACK), d_scale_got[:].rearrange("p (m t) -> p m t", t=PACK)
        )
        for j in range(4):
            nc.scalar.dma_start(d_scale[j:P:32, :].bitcast(I32), d_scale_dealt[8 * j : P : 32, :].bitcast(I32))

        d_word_got = work.tile([P, H], U32, name="d_word_got")
        nc.vector.tensor_copy(d_word_got[:], d_word_tab[:].indirect(k1_sb[:]))
        x_scale = reused.tile([P, S], U8, name="x_scale", align_bytes=64, offset=4 * N)
        nc.vector.tensor_copy(x_scale[:], x_scale_tab[:].indirect(offs_sb[:]))
        d_word = work.tile([P, H], U32, name="d_word", align_bytes=64)
        nc.vector.tensor_copy(
            d_word[:].rearrange("p (t m) -> p m t", t=PACK), d_word_got[:].rearrange("p (m t) -> p m t", t=PACK)
        )
        x_word = [work.tile([P, HALF], U32, name=f"x_word{u}", align_bytes=64) for u in range(2)]
        for u in range(2):
            nc.vector.tensor_copy(x_word[u][:], x_word_tab[:].indirect(entries(offs_sb, u * HALF, HALF)))

        w_word_raw = reused.tile([P, N], U32, name="w_word_raw", offset=0)
        nc.scalar.dma_start(w_word_raw[:].bitcast(I32), words_of(w1_words))
        w_word = work.tile([P, N], U32, name="w_word", align_bytes=64)
        nc.gpsimd.tensor_copy(
            w_word[:].rearrange("p (t m) -> p t m", t=PACK), w_word_raw[:].rearrange("p (m t) -> p t m", t=PACK)
        )
        w_scale = work.tile([P, N], U8, name="w_scale", align_bytes=64)
        nc.gpsimd.tensor_copy(
            w_scale[:].rearrange("p (t m) -> p t m", t=PACK), w_scale_raw[:].rearrange("p (m t) -> p t m", t=PACK)
        )

        h_ps = {}
        for pair in range(2):
            for u in range(2):
                for t in (2 * pair, 2 * pair + 1):
                    cols = slice(P * t, P * (t + 1))
                    h_ps[t, u] = psum.tile([P, HALF], F32, name=f"h_ps{t}{u}", tag=f"bank{t}{u}")
                    nc.tensor.matmul_mx(
                        out=h_ps[t, u][:], lhsT=d_word[:, cols].bitcast(FP8X4), lhsT_scale=d_scale[:, cols],
                        rhs=x_word[u][:].bitcast(FP8X4), rhs_scale=x_scale[:, u * HALF : (u + 1) * HALF], start=True, stop=True,
                    )

        h_sb = work.tile([P, PACK, S], F32, name="h_sb")
        h2_sb = [work.tile([P, S], F32, name=f"h2_sb{t}") for t in range(PACK)]
        pa = [work.tile([P, PACK, HALF], F32, name=f"pa{u}") for u in range(S // HALF)]
        chunks = S // Z_CHUNK
        h_sq = [work.tile([P, PACK, Z_CHUNK], F32, name=f"h_sq{c}") for c in range(chunks)]
        pa_sq = [work.tile([P, PACK, Z_CHUNK], F32, name=f"pa_sq{c}") for c in range(chunks)]
        den = [work.tile([P, PACK, Z_CHUNK], F32, name=f"den{c}") for c in range(chunks)]
        root = [work.tile([P, PACK, Z_CHUNK], F32, name=f"root{c}") for c in range(chunks)]
        inv = [work.tile([P, PACK, Z_CHUNK], F32, name=f"inv{c}") for c in range(chunks)]
        prod = [work.tile([P, PACK, Z_CHUNK], F32, name=f"prod{c}") for c in range(chunks)]
        h2_ps = {}

        def cols_of(c):
            return slice(c * Z_CHUNK, (c + 1) * Z_CHUNK)

        def pa_of(c):
            start = c * Z_CHUNK % HALF
            return pa[c * Z_CHUNK // HALF][:, :, start : start + Z_CHUNK]

        def fetch(t, u, on_vector):
            window = h_sb[:, t, :].indirect(entries(n1_sb, u * HALF, HALF))
            if on_vector:
                nc.vector.tensor_copy(pa[u][:, t, :], window)
            else:
                nc.scalar.activation(pa[u][:, t, :], window, ACT.Copy)

        def square_h(c):
            nc.scalar.activation(h_sq[c][:], h_sb[:, :, cols_of(c)], ACT.Square)

        def square_pa(c):
            nc.scalar.activation(pa_sq[c][:], pa_of(c), ACT.Square)

        def add_squares(c):
            nc.vector.tensor_tensor(den[c][:], h_sq[c][:], pa_sq[c][:], ALU.add)

        def inverse_root(c):
            nc.scalar.activation(root[c][:], den[c][:], ACT.Abs_reciprocal_sqrt, bias=64.0, scale=0.5)

        def inverse(c):
            nc.scalar.activation(inv[c][:], root[c][:], ACT.Square)

        def product(c):
            for t in range(PACK):
                nc.vector.scalar_tensor_tensor(
                    prod[c][:, t, :], h_sb[:, t, cols_of(c)], gain[:, t : t + 1], pa_of(c)[:, t, :], ALU.mult, ALU.mult
                )

        z = [work.tile([P, Z_CHUNK * PACK], BF16, name=f"z{c}", align_bytes=64) for c in range(chunks)]

        def round_z(c):
            nc.vector.tensor_tensor(
                z[c][:].rearrange("p (g i t) -> p g t i", i=4, t=PACK),
                prod[c][:].rearrange("p t (g i) -> p g t i", i=4),
                inv[c][:].rearrange("p t (g i) -> p g t i", i=4),
                ALU.mult,
            )

        def second_layer(c):
            z_word = work.tile([P, Z_CHUNK], U32, name=f"z_word{c}", align_bytes=64)
            z_scale = work.tile([P, Z_CHUNK], U8, name=f"z_scale{c}", align_bytes=64)
            nc.vector.quantize_mx(out=z_word[:].bitcast(FP8X4), scales=z_scale[:], in_=z[c][:])
            u, start = divmod(c * Z_CHUNK, HALF)
            for t in range(PACK):
                wc = slice(P * t, P * (t + 1))
                if start == 0:
                    h2_ps[t, u] = psum.tile([P, HALF], F32, name=f"h2_ps{t}{u}", tag=f"bank{t}{u}")
                nc.tensor.matmul_mx(
                    out=h2_ps[t, u][:, start : start + Z_CHUNK], lhsT=w_word[:, wc].bitcast(FP8X4), lhsT_scale=w_scale[:, wc],
                    rhs=z_word[:].bitcast(FP8X4), rhs_scale=z_scale[:], start=True, stop=True,
                )

        for pair in range(2):
            for t in (2 * pair, 2 * pair + 1):
                nc.scalar.copy(h_sb[:, t, 0:HALF], h_ps[t, 0][:])
            for t in (2 * pair, 2 * pair + 1):
                nc.vector.tensor_copy(h_sb[:, t, HALF:S], h_ps[t, 1][:])
            for t in (2 * pair, 2 * pair + 1):
                fetch(t, 0, True)
        square_h(0)
        square_h(1)
        for t in range(PACK):
            fetch(t, 1, t >= 2)
        square_pa(0)
        square_pa(1)
        add_squares(0)
        add_squares(1)
        square_h(2)
        square_h(3)
        square_pa(2)
        square_pa(3)
        inverse_root(0)
        add_squares(2)
        add_squares(3)
        for c in range(chunks):
            if c + 1 < chunks:
                inverse_root(c + 1)
            inverse(c)
            product(c)
            if c > 0:
                second_layer(c - 1)
            round_z(c)
        second_layer(chunks - 1)
        for t in range(PACK):
            nc.scalar.copy(h2_sb[t][:, 0:HALF], h2_ps[t, 0][:])
        for t in range(PACK):
            if t % 2 == 0:
                nc.scalar.copy(h2_sb[t][:, HALF:S], h2_ps[t, 1][:])
            else:
                nc.vector.tensor_copy(h2_sb[t][:, HALF:S], h2_ps[t, 1][:])

        out_rows = out_0.rearrange("(p t) j -> p t j", t=PACK)
        y_word = work.tile([P, S], U32, name="y_word", align_bytes=64)
        y_scale = work.tile([P, S], U8, name="y_scale", align_bytes=64)
        left = {}
        for u in range(2):
            for t in range(PACK):
                left[t, u] = work.tile([P, HALF], F32, name=f"left{t}{u}")
                window = h2_sb[t][:].indirect(entries(n2_sb, u * HALF, HALF))
                if (t, u) == (1, 0):
                    nc.vector.tensor_copy(left[t, u][:], window)
                else:
                    nc.scalar.activation(left[t, u][:], window, ACT.Copy)
        y = [work.tile([P, PACK, HALF], F32, name=f"y{u}") for u in range(2)]
        for u in range(2):
            for t in range(PACK):
                nc.vector.tensor_tensor(y[u][:, t, :], h2_sb[t][:].indirect(entries(n3_sb, u * HALF, HALF)), left[t, u][:], ALU.mult)
                if t % 2 == 1:
                    nc.sync.dma_start(out_rows[:, t - 1 : t + 1, u * HALF : (u + 1) * HALF], y[u][:, t - 1 : t + 1, :])
        for u in range(2):
            cols = slice(u * HALF, (u + 1) * HALF)
            y_bf = work.tile([P, HALF * PACK], BF16, name=f"y_bf{u}", align_bytes=64)
            woven = y_bf[:].rearrange("p (g i t) -> p g t i", i=4, t=PACK)
            planes = y[u][:].rearrange("p t (g i) -> p g t i", i=4)
            if u == 0:
                nc.scalar.copy(woven, planes)
            else:
                nc.vector.tensor_copy(woven[:, 0:48], planes[:, 0:48])
                nc.scalar.copy(woven[:, 48:64], planes[:, 48:64])
            nc.vector.quantize_mx(out=y_word[:, cols].bitcast(FP8X4), scales=y_scale[:, cols], in_=y_bf[:])
            nc.sync.dma_start(words_of(out_1)[:, cols], y_word[:, cols].bitcast(I32))
        for q in range(4):
            queue = nc.sync if q % 2 == 0 else nc.scalar
            queue.dma_start(out_2[0][4 * q : 4 * q + 4, :].bitcast(I32), y_scale[32 * q : 32 * q + 4, :].bitcast(I32))
